import numpy as np
import ml_dtypes


def mxq(x, axis, fmt="e4m3"):
    dtype, down = {"e4m3": (ml_dtypes.float8_e4m3fn, 7), "e5m2": (ml_dtypes.float8_e5m2, 14)}[fmt]
    v = np.moveaxis(np.asarray(x, np.float32).astype(ml_dtypes.bfloat16).astype(np.float64), axis, -1)
    blocks = v.reshape(v.shape[:-1] + (-1, 32))
    amax = np.abs(blocks).max(-1, keepdims=True)
    byte = np.maximum(np.where(amax > 0, np.frexp(amax)[1] - 1 + 127, 0) - down, 1)
    scale = np.exp2(byte - 127.0)
    codes = (blocks / scale).astype(np.float32).astype(dtype).astype(np.float64)
    return np.moveaxis((codes * scale).reshape(v.shape), -1, axis)


WIDE = False


def mx_kscale(k):
    if not WIDE:
        return np.ones(k)
    levels = np.array([10, -10, 5, -5, 0])
    if k % 512:
        return np.exp2(np.random.permutation(np.resize(levels, k // 32))).repeat(32)
    a = np.empty((k // 512, 16))
    for p in range(k // 512):
        a[p, :8] = np.random.permutation(np.resize(levels, 8))
        for g in range(8):
            far = levels[np.abs(levels - a[p, g]) >= 10]
            a[p, g + 8] = far[np.random.randint(len(far))]
    return np.exp2(a.ravel()).repeat(32)


def f64(x):
    return np.asarray(x).astype(np.float64)


def striped(idx):
    return np.tile(idx.reshape(-1, 16).T, (8, 1)).astype(np.uint16)


def unstriped(offs):
    return offs[:16].T.reshape(-1).astype(np.int64)


def striped8(idx):
    return np.concatenate([x.reshape(-1, 16).T for x in idx]).astype(np.uint16)


def runs(offs, k):
    lists = np.stack([offs[16 * r : 16 * r + 16].T.reshape(-1) for r in range(8)]).astype(np.int64)
    return lists[np.arange(k) % 512 // 64]


def pack_weight(w):
    k, n = w.shape
    w = f64(np.asarray(w, np.float32).astype(ml_dtypes.bfloat16)).reshape(k // 32, 32, n)
    amax = np.abs(w).max(1)
    byte = np.clip(np.where(amax > 0, np.frexp(amax)[1] - 1 + 127 - 7, 1), 1, 254)
    scaled = (w * np.exp2(127.0 - byte)[:, None, :]).reshape(k, n).astype(np.float32)
    words = np.ascontiguousarray(scaled.reshape(k // 512, 128, 4, n).transpose(0, 1, 3, 2)).astype(ml_dtypes.float8_e4m3fn).view(np.uint8)
    return words, np.ascontiguousarray(byte.astype(np.uint8).reshape(k // 512, 16, n))


def unpack_weight(words, scales):
    g, p, n, _ = words.shape
    vals = np.ascontiguousarray(words).view(ml_dtypes.float8_e4m3fn).astype(np.float64) * np.repeat(np.exp2(scales.astype(np.float64) - 127.0), 8, axis=1)[..., None]
    return vals.transpose(0, 1, 3, 2).reshape(g * 512, n)


K, T, S, H, C, W = 512, 2048, 256, 512, 512, 128


def setup_inputs():
    n = np.random.standard_normal
    s = mx_kscale(K)[:, None]
    packed_xT = pack_weight(n((K, T)) * s)
    perm = np.random.permutation(S)
    return {
        "x_words": packed_xT[0],
        "x_scales": packed_xT[1],
        "w1": (n((K, H)) / np.sqrt(2 * K) / s).astype(np.float32),
        "w2": (n((K, H)) / np.sqrt(2 * K) / s).astype(np.float32),
        "gs": (np.random.uniform(0.5, 1.5, (K, 1)) / s).astype(np.float32),
        "offs": striped(np.random.permutation(T)[:S]),
        "hz": striped8(np.random.randint(0, T, (8, S))),
        "n1": striped(np.random.permutation(S)),
        "n2": striped(np.random.permutation(S)),
        "cand": striped8(np.random.randint(0, T, (8, C))),
        "n3": striped(perm[:W]),
        "n4": striped(perm[W:]),
    }


def reference(x_words, x_scales, w1, w2, gs, offs, hz, n1, n2, cand, n3, n4):
    x_cand = unpack_weight(x_words, x_scales)[np.arange(K)[:, None], runs(cand, K)]
    xq = unpack_weight(x_words, x_scales)[:, unstriped(offs)]
    x_hz = unpack_weight(x_words, x_scales)[np.arange(K)[:, None], runs(hz, K)]
    y = mxq(f64(w1), 0, "e4m3").T @ xq + mxq(f64(w2), 0, "e4m3").T @ x_hz
    ds = np.zeros((H, S))
    ds[:, unstriped(n1)] = y
    st = np.maximum(y, ds)
    ds2 = np.zeros((H, S))
    ds2[:, unstriped(n2)] = st
    z = f64(gs) * (st - ds2)
    s = 0.0625 * ((x_cand.T @ mxq(z, 0, "e4m3")))
    pa = s[:, unstriped(n3)]
    pb = s[:, unstriped(n4)]
    ra = np.maximum(pa, pb)
    out = s.copy()
    out[:, unstriped(n3)] = ra
    return out

@@ -1,0 +1,249 @@
+from contextlib import ExitStack
+
+import concourse.mybir as mybir
+
+K, T, S, H, C, W = 512, 2048, 256, 512, 512, 128
+FLOPS = 2 * K * H * S * 2 + 2 * K * C * S
+
+F32 = mybir.dt.float32
+BF16 = mybir.dt.bfloat16
+I32 = mybir.dt.int32
+U32 = mybir.dt.uint32
+U16 = mybir.dt.uint16
+U8 = mybir.dt.uint8
+FP8X4 = mybir.dt.float8_e4m3fn_x4
+ALU = mybir.AluOpType
+COPY = mybir.ActivationFunctionType.Copy
+
+P = 128
+PACK = 4
+HALF = P // 2
+WINDOW = 2 * S
+
+
+def tile_picked_dthzksndtwinfill_none_p_kernel(
+    tc, x_words, x_scales, w1, w2, gs, offs, hz, n1, n2, cand, n3, n4, out
+):
+    nc = tc.nc
+    with ExitStack() as ctx:
+        lists = ctx.enter_context(tc.tile_pool(name="lists", bufs=1))
+        keep = ctx.enter_context(tc.tile_pool(name="keep", bufs=1))
+        psum = ctx.enter_context(tc.psum_pool(name="psum", bufs=1))
+
+        def load_list(name, src):
+            held = lists.tile(list(src.shape), U16, name=name)
+            nc.sync.dma_start(held[:], src)
+            return held
+
+        def load_half(name, w, half):
+            raw = keep.tile([P, PACK, S], F32, name=name)
+            cols = slice(half * S, (half + 1) * S)
+            nc.sync.dma_start(raw[:], w.rearrange("(p j) c -> p j c", j=PACK)[:, :, cols])
+            return raw
+
+        gs_t = keep.tile([P, PACK], F32, name="gs_t")
+        nc.scalar.dma_start(gs_t[:], gs.rearrange("(p t) o -> p (t o)", t=PACK))
+        gain = keep.tile([P, PACK], F32, name="gain")
+        nc.scalar.activation(gain[:], gs_t[:], COPY, scale=0.0625)
+        scale_rows = keep.tile([P, T], U8, name="scale_rows")
+        nc.vector.memset(scale_rows[:].bitcast(I32), 0)
+        for e in range(2):
+            nc.scalar.dma_start(
+                scale_rows[e:P:16, :].bitcast(I32), x_scales[0, e:16:2, :].bitcast(I32)
+            )
+        hz_t = load_list("hz_t", hz)
+        offs_t = load_list("offs_t", offs)
+        words = keep.tile([P, T], I32, name="words")
+        nc.sync.dma_start(words[:], x_words[0].rearrange("p n t -> p (n t)").bitcast(I32))
+        w1_lo = load_half("w1_raw", w1, 0)
+        n1_t = load_list("n1_t", n1)
+        n2_t = load_list("n2_t", n2)
+        w2_lo = load_half("w2_raw", w2, 0)
+        cand_t = load_list("cand_t", cand)
+        n3_t = load_list("n3_t", n3)
+        n4_t = load_list("n4_t", n4)
+
+        def place_scales(name, picked, queue):
+            width = picked.shape[1]
+            placed = keep.tile([P, width], U8, name=name, align_bytes=64)
+            nc.vector.tensor_copy(placed[:].bitcast(I32), picked[:].bitcast(I32))
+            for e in range(2):
+                queue.dma_start(
+                    placed[2 + e : P : 32, :].bitcast(I32), picked[16 + e : P : 32, :].bitcast(I32)
+                )
+            return placed
+
+        tok_bytes = keep.tile([P, 2 * S], U8, name="tok_bytes", align_bytes=64)
+        nc.vector.tensor_copy(tok_bytes[:, S:], scale_rows[:].indirect(hz_t[:]))
+        nc.vector.tensor_copy(tok_bytes[:, :S], scale_rows[:].indirect(offs_t[:]))
+        tok_scales = place_scales("tok_scales", tok_bytes, nc.scalar)
+
+
+        xq = keep.tile([P, S], U32, name="xq", align_bytes=64)
+        nc.vector.tensor_copy(xq[:], words[:].bitcast(U32).indirect(offs_t[:]))
+        xh = keep.tile([P, S], U32, name="xh", align_bytes=64)
+        nc.vector.tensor_copy(xh[:], words[:].bitcast(U32).indirect(hz_t[:]))
+
+        grouped = {}
+        codes = {}
+        wscale = {}
+        for i in range(2):
+            for name, width in (("a", P), ("r", 3 * P)):
+                grouped[i, name] = keep.tile([P, width * PACK], BF16, name="g%d%s" % (i, name), align_bytes=64)
+                codes[i, name] = keep.tile([P, width], U32, name="c%d%s" % (i, name), align_bytes=64)
+                wscale[i, name] = keep.tile([P, width], U8, name="s%d%s" % (i, name), align_bytes=64)
+
+        def quant(i, name):
+            nc.vector.quantize_mx(out=codes[i, name][:].bitcast(FP8X4), scales=wscale[i, name][:], in_=grouped[i, name][:])
+
+        def by_slot(raw):
+            return raw[:].rearrange("p j (m t) -> p m t j", t=PACK)
+
+        def cast_cd(i, raw, half, engine):
+            dst = grouped[i, "r"][:, P * PACK :].rearrange("p (t m j) -> p m t j", t=2, j=PACK)[:, half * HALF : (half + 1) * HALF]
+            src = by_slot(raw)[:, :, 2:4, :]
+            if engine == "scalar":
+                nc.scalar.activation(dst, src, COPY)
+            else:
+                nc.vector.tensor_copy(dst, src)
+
+        for i, raw in ((0, w1_lo), (1, w2_lo)):
+            nc.vector.tensor_copy(
+                grouped[i, "a"][:].rearrange("p (t m j) -> p m t j", t=2, j=PACK), by_slot(raw)[:, :, 0:2, :]
+            )
+            quant(i, "a")
+            cast_cd(i, raw, 0, "scalar")
+
+        moving = ((xq, slice(0, S)), (xh, slice(S, 2 * S)))
+
+        def product(r, name, cols):
+            acc = psum.tile([P, S], F32, name="y_acc%d" % r)
+            for i in range(2):
+                nc.tensor.matmul_mx(
+                    out=acc[:],
+                    lhsT=codes[i, name][:, cols].bitcast(FP8X4),
+                    lhsT_scale=wscale[i, name][:, cols],
+                    rhs=moving[i][0][:].bitcast(FP8X4),
+                    rhs_scale=tok_scales[:, moving[i][1]],
+                    start=(i == 0),
+                    stop=(i == 1),
+                )
+            y = keep.tile([P, S], F32, name="y%d" % r)
+            if r == 0:
+                nc.scalar.activation(y[:], acc[:], COPY)
+            else:
+                nc.vector.tensor_copy(y[:], acc[:])
+            return y
+
+        st = {}
+        diff = {}
+
+        def step1(r, y):
+            ds = keep.tile([P, WINDOW], F32, name="ds%d" % r)
+            nc.scalar.activation(ds[:].indirect(n1_t[:]), y[:], COPY)
+            st[r] = keep.tile([P, S], F32, name="st%d" % r)
+            nc.vector.tensor_tensor(st[r][:], ds[:, :S], y[:], ALU.max)
+
+        def step2(r, pieces, tag):
+            ds2 = keep.tile([P, WINDOW], F32, name="ds2_%d" % r)
+            nc.scalar.activation(ds2[:].indirect(n2_t[:]), st[r][:], COPY)
+            diff[r] = keep.tile([P, S], F32, name="diff%d" % r, tag=tag, align_bytes=64)
+            for h in range(pieces):
+                cols = slice(h * S // pieces, (h + 1) * S // pieces)
+                nc.vector.tensor_tensor(diff[r][:, cols], st[r][:, cols], ds2[:, cols], ALU.subtract)
+
+        zb = keep.tile([P, S, PACK], BF16, name="zb", align_bytes=64)
+
+        def weigh(src, slot, rows, cols):
+            nc.vector.tensor_scalar(zb[rows, cols, slot], src[rows, cols], gain[rows, slot : slot + 1], None, ALU.mult)
+
+        every = slice(0, P)
+        allc = slice(0, S)
+        lo = slice(0, HALF)
+        hi = slice(HALF, P)
+
+        y0 = product(0, "a", slice(0, P))
+        step1(0, y0)
+
+        w1_hi = load_half("w1_raw", w1, 1)
+        w2_hi = load_half("w2_raw", w2, 1)
+        for i, raw in ((0, w1_hi), (1, w2_hi)):
+            nc.vector.tensor_copy(
+                grouped[i, "r"][:, : P * PACK].rearrange("p (t m j) -> p m t j", t=2, j=PACK), by_slot(raw)[:, :, 0:2, :]
+            )
+            cast_cd(i, raw, 1, "vector")
+            quant(i, "r")
+        ys = [product(r, "r", slice((r - 1) * P, r * P)) for r in (1, 2, 3)]
+
+        step2(0, 1, "xh")
+        moved_lo = keep.tile([P, S], F32, name="moved_lo", align_bytes=64)
+        nc.sync.dma_start(moved_lo[lo, :], diff[0][hi, :])
+        weigh(diff[0], 0, lo, allc)
+
+        cand_bytes = keep.tile([P, C], U8, name="cand_bytes", tag="s1r", align_bytes=64)
+        nc.vector.tensor_copy(cand_bytes[:], scale_rows[:].indirect(cand_t[:]))
+        cand_scales = place_scales("cand_scales", cand_bytes, nc.sync)
+        xc = keep.tile([P, C], U32, name="xc", tag="c1r", align_bytes=64)
+        nc.vector.tensor_copy(xc[:], words[:].bitcast(U32).indirect(cand_t[:]))
+        weigh(moved_lo, 1, lo, allc)
+
+        for r in (1, 2, 3):
+            step1(r, ys[r - 1])
+        step2(1, 1, "diff1")
+        moved_hi = keep.tile([P, S], F32, name="moved_hi", align_bytes=64)
+        nc.sync.dma_start(moved_hi[hi, :], diff[1][lo, :])
+        weigh(diff[1], 1, hi, allc)
+        step2(2, 1, "diff2")
+        weigh(diff[2], 2, every, allc)
+        weigh(moved_hi, 0, hi, allc)
+        step2(3, 2, "moved_hi")
+        zq = keep.tile([P, S], U32, name="zq", align_bytes=64)
+        zs = keep.tile([P, S], U8, name="zs", align_bytes=64)
+        halves = (slice(0, S // 2), slice(S // 2, S))
+        for cols in halves:
+            weigh(diff[3], 3, every, cols)
+        for cols in halves:
+            nc.vector.quantize_mx(
+                out=zq[:, cols].bitcast(FP8X4), scales=zs[:, cols], in_=zb[:, cols, :].rearrange("p n t -> p (n t)")
+            )
+
+        score = []
+        for c in range(C // P):
+            rows = slice(c * P, (c + 1) * P)
+            acc = psum.tile([P, S], F32, name="s_acc%d" % c)
+            for cols in halves if c == 0 else (allc,):
+                nc.tensor.matmul_mx(
+                    out=acc[:, cols],
+                    lhsT=xc[:, rows].bitcast(FP8X4),
+                    lhsT_scale=cand_scales[:, rows],
+                    rhs=zq[:, cols].bitcast(FP8X4),
+                    rhs_scale=zs[:, cols],
+                    start=True,
+                    stop=True,
+                )
+            s = keep.tile([P, S], F32, name="score%d" % c)
+            if c == 0:
+                nc.scalar.activation(s[:], acc[:], COPY)
+            else:
+                nc.vector.tensor_copy(s[:], acc[:])
+            score.append(s)
+
+        larger = {}
+
+        def pair_up(c):
+            pa = keep.tile([P, W], F32, name="pa%d" % c)
+            pb = keep.tile([P, W], F32, name="pb%d" % c)
+            nc.scalar.activation(pa[:], score[c][:].indirect(n3_t[:]), COPY)
+            nc.scalar.activation(pb[:], score[c][:].indirect(n4_t[:]), COPY)
+            larger[c] = keep.tile([P, W], F32, name="larger%d" % c)
+            nc.vector.tensor_tensor(larger[c][:], pa[:], pb[:], ALU.max)
+
+        def put_back(c):
+            nc.scalar.activation(score[c][:].indirect(n3_t[:]), larger[c][:], COPY)
+            nc.sync.dma_start(out[c * P : (c + 1) * P, :], score[c][:])
+
+        pair_up(0)
+        for c in range(1, C // P):
+            pair_up(c)
+            put_back(c - 1)
+        put_back(C // P - 1)

@@ -35,8 +35,8 @@ def tile_picked_dthzksndtwinfill_none_p_kernel(
             nc.sync.dma_start(held[:], src)
             return held
 
-        def load_half(name, w, half):
-            raw = keep.tile([P, PACK, S], F32, name=name)
+        def load_half(name, tag, w, half):
+            raw = keep.tile([P, PACK, S], F32, name=name, tag=tag, align_bytes=64)
             cols = slice(half * S, (half + 1) * S)
             nc.sync.dma_start(raw[:], w.rearrange("(p j) c -> p j c", j=PACK)[:, :, cols])
             return raw
@@ -44,21 +44,21 @@ def tile_picked_dthzksndtwinfill_none_p_kernel(
         gs_t = keep.tile([P, PACK], F32, name="gs_t")
         nc.scalar.dma_start(gs_t[:], gs.rearrange("(p t) o -> p (t o)", t=PACK))
         gain = keep.tile([P, PACK], F32, name="gain")
-        nc.scalar.activation(gain[:], gs_t[:], COPY, scale=0.0625)
+        nc.scalar.activation(gain[:], gs_t[:], COPY, scale=-0.0625)
         scale_rows = keep.tile([P, T], U8, name="scale_rows")
         nc.vector.memset(scale_rows[:].bitcast(I32), 0)
-        for e in range(2):
-            nc.scalar.dma_start(
-                scale_rows[e:P:16, :].bitcast(I32), x_scales[0, e:16:2, :].bitcast(I32)
-            )
         hz_t = load_list("hz_t", hz)
         offs_t = load_list("offs_t", offs)
-        words = keep.tile([P, T], I32, name="words")
-        nc.sync.dma_start(words[:], x_words[0].rearrange("p n t -> p (n t)").bitcast(I32))
-        w1_lo = load_half("w1_raw", w1, 0)
         n1_t = load_list("n1_t", n1)
         n2_t = load_list("n2_t", n2)
-        w2_lo = load_half("w2_raw", w2, 0)
+        for e in range(2):
+            nc.sync.dma_start(
+                scale_rows[e:P:16, :].bitcast(I32), x_scales[0, e:16:2, :].bitcast(I32)
+            )
+        w1_lo = load_half("w1_lo", "w1_raw", w1, 0)
+        words = keep.tile([P, T], I32, name="words")
+        nc.sync.dma_start(words[:], x_words[0].rearrange("p n t -> p (n t)").bitcast(I32))
+        w2_lo = load_half("w2_lo", "w2_raw", w2, 0)
         cand_t = load_list("cand_t", cand)
         n3_t = load_list("n3_t", n3)
         n4_t = load_list("n4_t", n4)
@@ -88,7 +88,7 @@ def tile_picked_dthzksndtwinfill_none_p_kernel(
         codes = {}
         wscale = {}
         for i in range(2):
-            for name, width in (("a", P), ("r", 3 * P)):
+            for name, width in (("a", P), ("b", P), ("r", 2 * P)):
                 grouped[i, name] = keep.tile([P, width * PACK], BF16, name="g%d%s" % (i, name), align_bytes=64)
                 codes[i, name] = keep.tile([P, width], U32, name="c%d%s" % (i, name), align_bytes=64)
                 wscale[i, name] = keep.tile([P, width], U8, name="s%d%s" % (i, name), align_bytes=64)
@@ -100,27 +100,37 @@ def tile_picked_dthzksndtwinfill_none_p_kernel(
             return raw[:].rearrange("p j (m t) -> p m t j", t=PACK)
 
         def cast_cd(i, raw, half, engine):
-            dst = grouped[i, "r"][:, P * PACK :].rearrange("p (t m j) -> p m t j", t=2, j=PACK)[:, half * HALF : (half + 1) * HALF]
+            dst = grouped[i, "r"][:].rearrange("p (t m j) -> p m t j", t=2, j=PACK)[:, half * HALF : (half + 1) * HALF]
             src = by_slot(raw)[:, :, 2:4, :]
             if engine == "scalar":
                 nc.scalar.activation(dst, src, COPY)
             else:
                 nc.vector.tensor_copy(dst, src)
 
-        for i, raw in ((0, w1_lo), (1, w2_lo)):
-            nc.vector.tensor_copy(
-                grouped[i, "a"][:].rearrange("p (t m j) -> p m t j", t=2, j=PACK), by_slot(raw)[:, :, 0:2, :]
-            )
-            quant(i, "a")
-            cast_cd(i, raw, 0, "scalar")
+        def pair_view(i, name):
+            return grouped[i, name][:].rearrange("p (t m j) -> p m t j", t=2, j=PACK)
+
+        nc.vector.tensor_copy(pair_view(0, "a"), by_slot(w1_lo)[:, :, 0:2, :])
+        quant(0, "a")
+        cast_cd(0, w1_lo, 0, "scalar")
+        nc.vector.tensor_copy(pair_view(1, "a")[:, :, 0, :], by_slot(w2_lo)[:, :, 0, :])
+        nc.scalar.activation(pair_view(1, "a")[:, :, 1, :], by_slot(w2_lo)[:, :, 1, :], COPY)
+        quant(1, "a")
+        cast_cd(1, w2_lo, 0, "scalar")
 
         moving = ((xq, slice(0, S)), (xh, slice(S, 2 * S)))
+        acc_y = {}
+        y = {}
+        ds = {}
+        st = {}
+        ds2 = {}
+        diff = {}
 
         def product(r, name, cols):
-            acc = psum.tile([P, S], F32, name="y_acc%d" % r)
+            acc_y[r] = psum.tile([P, S], F32, name="y_acc%d" % r)
             for i in range(2):
                 nc.tensor.matmul_mx(
-                    out=acc[:],
+                    out=acc_y[r][:],
                     lhsT=codes[i, name][:, cols].bitcast(FP8X4),
                     lhsT_scale=wscale[i, name][:, cols],
                     rhs=moving[i][0][:].bitcast(FP8X4),
@@ -128,29 +138,31 @@ def tile_picked_dthzksndtwinfill_none_p_kernel(
                     start=(i == 0),
                     stop=(i == 1),
                 )
-            y = keep.tile([P, S], F32, name="y%d" % r)
+
+        def evacuate(r, tag):
+            y[r] = keep.tile([P, S], F32, name="y%d" % r, tag=tag, align_bytes=64)
             if r == 0:
-                nc.scalar.activation(y[:], acc[:], COPY)
+                nc.scalar.activation(y[r][:], acc_y[r][:], COPY)
             else:
-                nc.vector.tensor_copy(y[:], acc[:])
-            return y
+                nc.vector.tensor_copy(y[r][:], acc_y[r][:])
 
-        st = {}
-        diff = {}
+        def send1(r):
+            ds[r] = keep.tile([P, WINDOW], F32, name="ds%d" % r, align_bytes=64)
+            nc.scalar.activation(ds[r][:].indirect(n1_t[:]), y[r][:], COPY)
 
-        def step1(r, y):
-            ds = keep.tile([P, WINDOW], F32, name="ds%d" % r)
-            nc.scalar.activation(ds[:].indirect(n1_t[:]), y[:], COPY)
-            st[r] = keep.tile([P, S], F32, name="st%d" % r)
-            nc.vector.tensor_tensor(st[r][:], ds[:, :S], y[:], ALU.max)
+        def larger_of(r, tag):
+            st[r] = keep.tile([P, S], F32, name="st%d" % r, tag=tag, align_bytes=64)
+            nc.vector.tensor_tensor(st[r][:], ds[r][:, :S], y[r][:], ALU.max)
 
-        def step2(r, pieces, tag):
-            ds2 = keep.tile([P, WINDOW], F32, name="ds2_%d" % r)
-            nc.scalar.activation(ds2[:].indirect(n2_t[:]), st[r][:], COPY)
+        def send2(r):
+            ds2[r] = keep.tile([P, WINDOW], F32, name="ds2_%d" % r, align_bytes=64)
+            nc.scalar.activation(ds2[r][:].indirect(n2_t[:]), st[r][:], COPY)
+
+        def subtract(r, pieces, tag):
             diff[r] = keep.tile([P, S], F32, name="diff%d" % r, tag=tag, align_bytes=64)
             for h in range(pieces):
                 cols = slice(h * S // pieces, (h + 1) * S // pieces)
-                nc.vector.tensor_tensor(diff[r][:, cols], st[r][:, cols], ds2[:, cols], ALU.subtract)
+                nc.vector.tensor_tensor(diff[r][:, cols], ds2[r][:, cols], st[r][:, cols], ALU.subtract)
 
         zb = keep.tile([P, S, PACK], BF16, name="zb", align_bytes=64)
 
@@ -162,69 +174,92 @@ def tile_picked_dthzksndtwinfill_none_p_kernel(
         lo = slice(0, HALF)
         hi = slice(HALF, P)
 
-        y0 = product(0, "a", slice(0, P))
-        step1(0, y0)
+        product(0, "a", slice(0, P))
+        evacuate(0, "y0")
+        send1(0)
 
-        w1_hi = load_half("w1_raw", w1, 1)
-        w2_hi = load_half("w2_raw", w2, 1)
+        w1_hi = load_half("w1_hi", "w1_raw", w1, 1)
+        w2_hi = load_half("w2_hi", "tok_bytes", w2, 1)
         for i, raw in ((0, w1_hi), (1, w2_hi)):
-            nc.vector.tensor_copy(
-                grouped[i, "r"][:, : P * PACK].rearrange("p (t m j) -> p m t j", t=2, j=PACK), by_slot(raw)[:, :, 0:2, :]
-            )
+            nc.vector.tensor_copy(pair_view(i, "b"), by_slot(raw)[:, :, 0:2, :])
+            quant(i, "b")
+        larger_of(0, "g1b")
+        send2(0)
+        product(1, "b", slice(0, P))
+        evacuate(1, "y1")
+        for i, raw in ((0, w1_hi), (1, w2_hi)):
             cast_cd(i, raw, 1, "vector")
             quant(i, "r")
-        ys = [product(r, "r", slice((r - 1) * P, r * P)) for r in (1, 2, 3)]
+        product(2, "r", slice(0, P))
+        product(3, "r", slice(P, 2 * P))
+        evacuate(2, "y2")
+        send1(1)
+        send1(2)
 
-        step2(0, 1, "xh")
+        subtract(0, 1, "xh")
         moved_lo = keep.tile([P, S], F32, name="moved_lo", align_bytes=64)
         nc.sync.dma_start(moved_lo[lo, :], diff[0][hi, :])
         weigh(diff[0], 0, lo, allc)
-
         cand_bytes = keep.tile([P, C], U8, name="cand_bytes", tag="s1r", align_bytes=64)
         nc.vector.tensor_copy(cand_bytes[:], scale_rows[:].indirect(cand_t[:]))
         cand_scales = place_scales("cand_scales", cand_bytes, nc.sync)
+
+        larger_of(1, "tok_scales")
+        evacuate(3, "ds1")
+        send2(1)
+        send1(3)
         xc = keep.tile([P, C], U32, name="xc", tag="c1r", align_bytes=64)
         nc.vector.tensor_copy(xc[:], words[:].bitcast(U32).indirect(cand_t[:]))
         weigh(moved_lo, 1, lo, allc)
+        larger_of(2, "st2")
 
-        for r in (1, 2, 3):
-            step1(r, ys[r - 1])
-        step2(1, 1, "diff1")
+        subtract(1, 1, "diff1")
         moved_hi = keep.tile([P, S], F32, name="moved_hi", align_bytes=64)
         nc.sync.dma_start(moved_hi[hi, :], diff[1][lo, :])
         weigh(diff[1], 1, hi, allc)
-        step2(2, 1, "diff2")
-        weigh(diff[2], 2, every, allc)
+        larger_of(3, "st3")
+        send2(2)
+        send2(3)
+        st3_weighed = keep.tile([P, S], F32, name="st3_weighed", align_bytes=64)
+        nc.vector.tensor_scalar(st3_weighed[:], st[3][:], gain[:, 3:4], None, ALU.mult)
         weigh(moved_hi, 0, hi, allc)
-        step2(3, 2, "moved_hi")
+        subtract(2, 1, "moved_hi")
+        weigh(diff[2], 2, every, allc)
         zq = keep.tile([P, S], U32, name="zq", align_bytes=64)
         zs = keep.tile([P, S], U8, name="zs", align_bytes=64)
         halves = (slice(0, S // 2), slice(S // 2, S))
         for cols in halves:
-            weigh(diff[3], 3, every, cols)
+            nc.vector.scalar_tensor_tensor(
+                zb[:, cols, 3], ds2[3][:, cols], gain[:, 3:4], st3_weighed[:, cols], ALU.mult, ALU.subtract
+            )
         for cols in halves:
             nc.vector.quantize_mx(
                 out=zq[:, cols].bitcast(FP8X4), scales=zs[:, cols], in_=zb[:, cols, :].rearrange("p n t -> p (n t)")
             )
 
+        def scores(acc, rows, cols):
+            nc.tensor.matmul_mx(
+                out=acc,
+                lhsT=xc[:, rows].bitcast(FP8X4),
+                lhsT_scale=cand_scales[:, rows],
+                rhs=zq[:, cols].bitcast(FP8X4),
+                rhs_scale=zs[:, cols],
+                start=True,
+                stop=True,
+            )
+
         score = []
         for c in range(C // P):
             rows = slice(c * P, (c + 1) * P)
-            acc = psum.tile([P, S], F32, name="s_acc%d" % c)
-            for cols in halves if c == 0 else (allc,):
-                nc.tensor.matmul_mx(
-                    out=acc[:, cols],
-                    lhsT=xc[:, rows].bitcast(FP8X4),
-                    lhsT_scale=cand_scales[:, rows],
-                    rhs=zq[:, cols].bitcast(FP8X4),
-                    rhs_scale=zs[:, cols],
-                    start=True,
-                    stop=True,
-                )
             s = keep.tile([P, S], F32, name="score%d" % c)
             if c == 0:
-                nc.scalar.activation(s[:], acc[:], COPY)
+                for h, cols in enumerate(halves):
+                    acc = psum.tile([P, S // 2], F32, name="s_half%d" % h, tag="y_acc%d" % h)
+                    scores(acc[:], rows, cols)
+                    nc.scalar.activation(s[:, cols], acc[:], COPY)
             else:
+                acc = psum.tile([P, S], F32, name="s_acc%d" % c)
+                scores(acc[:], rows, allc)
                 nc.vector.tensor_copy(s[:], acc[:])
             score.append(s)
 
@@ -240,7 +275,8 @@ def tile_picked_dthzksndtwinfill_none_p_kernel(
 
         def put_back(c):
             nc.scalar.activation(score[c][:].indirect(n3_t[:]), larger[c][:], COPY)
-            nc.sync.dma_start(out[c * P : (c + 1) * P, :], score[c][:])
+            queue = nc.scalar if c == C // P - 1 else nc.sync
+            queue.dma_start(out[c * P : (c + 1) * P, :], score[c][:])
 
         pair_up(0)
         for c in range(1, C // P):

@@ -35,30 +35,26 @@ def tile_picked_dthzksndtwinfill_none_p_kernel(
             nc.sync.dma_start(held[:], src)
             return held
 
-        def load_half(name, tag, w, half):
+        def load_half(name, tag, w, half, queue):
             raw = keep.tile([P, PACK, S], F32, name=name, tag=tag, align_bytes=64)
             cols = slice(half * S, (half + 1) * S)
-            nc.sync.dma_start(raw[:], w.rearrange("(p j) c -> p j c", j=PACK)[:, :, cols])
+            queue.dma_start(raw[:], w.rearrange("(p j) c -> p j c", j=PACK)[:, :, cols])
             return raw
 
-        gs_t = keep.tile([P, PACK], F32, name="gs_t")
-        nc.scalar.dma_start(gs_t[:], gs.rearrange("(p t) o -> p (t o)", t=PACK))
-        gain = keep.tile([P, PACK], F32, name="gain")
-        nc.scalar.activation(gain[:], gs_t[:], COPY, scale=-0.0625)
+        w1_lo = load_half("w1_lo", "w1_raw", w1, 0, nc.scalar)
         scale_rows = keep.tile([P, T], U8, name="scale_rows")
         nc.vector.memset(scale_rows[:].bitcast(I32), 0)
         hz_t = load_list("hz_t", hz)
         offs_t = load_list("offs_t", offs)
         n1_t = load_list("n1_t", n1)
-        n2_t = load_list("n2_t", n2)
         for e in range(2):
             nc.sync.dma_start(
                 scale_rows[e:P:16, :].bitcast(I32), x_scales[0, e:16:2, :].bitcast(I32)
             )
-        w1_lo = load_half("w1_lo", "w1_raw", w1, 0)
         words = keep.tile([P, T], I32, name="words")
         nc.sync.dma_start(words[:], x_words[0].rearrange("p n t -> p (n t)").bitcast(I32))
-        w2_lo = load_half("w2_lo", "w2_raw", w2, 0)
+        w2_lo = load_half("w2_lo", "w2_raw", w2, 0, nc.sync)
+        n2_t = load_list("n2_t", n2)
         cand_t = load_list("cand_t", cand)
         n3_t = load_list("n3_t", n3)
         n4_t = load_list("n4_t", n4)
@@ -69,14 +65,14 @@ def tile_picked_dthzksndtwinfill_none_p_kernel(
             nc.vector.tensor_copy(placed[:].bitcast(I32), picked[:].bitcast(I32))
             for e in range(2):
                 queue.dma_start(
-                    placed[2 + e : P : 32, :].bitcast(I32), picked[16 + e : P : 32, :].bitcast(I32)
+                    placed[2 + e : P : 32, :].bitcast(I32), placed[16 + e : P : 32, :].bitcast(I32)
                 )
             return placed
 
         tok_bytes = keep.tile([P, 2 * S], U8, name="tok_bytes", align_bytes=64)
         nc.vector.tensor_copy(tok_bytes[:, S:], scale_rows[:].indirect(hz_t[:]))
         nc.vector.tensor_copy(tok_bytes[:, :S], scale_rows[:].indirect(offs_t[:]))
-        tok_scales = place_scales("tok_scales", tok_bytes, nc.scalar)
+        tok_scales = place_scales("tok_scales", tok_bytes, nc.sync)
 
 
         xq = keep.tile([P, S], U32, name="xq", align_bytes=64)
@@ -89,8 +85,10 @@ def tile_picked_dthzksndtwinfill_none_p_kernel(
         wscale = {}
         for i in range(2):
             for name, width in (("a", P), ("b", P), ("r", 2 * P)):
-                grouped[i, name] = keep.tile([P, width * PACK], BF16, name="g%d%s" % (i, name), align_bytes=64)
-                codes[i, name] = keep.tile([P, width], U32, name="c%d%s" % (i, name), align_bytes=64)
+                if name != "a":
+                    grouped[i, name] = keep.tile([P, width * PACK], BF16, name="g%d%s" % (i, name), align_bytes=64)
+                tag = "tok_bytes" if (i, name) == (0, "a") else "c%d%s" % (i, name)
+                codes[i, name] = keep.tile([P, width], U32, name="c%d%s" % (i, name), tag=tag, align_bytes=64)
                 wscale[i, name] = keep.tile([P, width], U8, name="s%d%s" % (i, name), align_bytes=64)
 
         def quant(i, name):
@@ -110,13 +108,20 @@ def tile_picked_dthzksndtwinfill_none_p_kernel(
         def pair_view(i, name):
             return grouped[i, name][:].rearrange("p (t m j) -> p m t j", t=2, j=PACK)
 
-        nc.vector.tensor_copy(pair_view(0, "a"), by_slot(w1_lo)[:, :, 0:2, :])
-        quant(0, "a")
-        cast_cd(0, w1_lo, 0, "scalar")
-        nc.vector.tensor_copy(pair_view(1, "a")[:, :, 0, :], by_slot(w2_lo)[:, :, 0, :])
-        nc.scalar.activation(pair_view(1, "a")[:, :, 1, :], by_slot(w2_lo)[:, :, 1, :], COPY)
-        quant(1, "a")
-        cast_cd(1, w2_lo, 0, "scalar")
+        for i, raw in ((0, w1_lo), (1, w2_lo)):
+            for t in range(2):
+                one = keep.tile([P, HALF, PACK], BF16, name="g%da%d" % (i, t), align_bytes=64)
+                if (i, t) == (1, 0):
+                    nc.vector.tensor_copy(one[:], by_slot(raw)[:, :, t, :])
+                else:
+                    nc.scalar.activation(one[:], by_slot(raw)[:, :, t, :], COPY)
+                cols = slice(t * HALF, (t + 1) * HALF)
+                nc.vector.quantize_mx(
+                    out=codes[i, "a"][:, cols].bitcast(FP8X4),
+                    scales=wscale[i, "a"][:, cols],
+                    in_=one[:].rearrange("p m j -> p (m j)"),
+                )
+            cast_cd(i, raw, 0, "scalar")
 
         moving = ((xq, slice(0, S)), (xh, slice(S, 2 * S)))
         acc_y = {}
@@ -141,10 +146,7 @@ def tile_picked_dthzksndtwinfill_none_p_kernel(
 
         def evacuate(r, tag):
             y[r] = keep.tile([P, S], F32, name="y%d" % r, tag=tag, align_bytes=64)
-            if r == 0:
-                nc.scalar.activation(y[r][:], acc_y[r][:], COPY)
-            else:
-                nc.vector.tensor_copy(y[r][:], acc_y[r][:])
+            nc.vector.tensor_copy(y[r][:], acc_y[r][:])
 
         def send1(r):
             ds[r] = keep.tile([P, WINDOW], F32, name="ds%d" % r, align_bytes=64)
@@ -174,14 +176,29 @@ def tile_picked_dthzksndtwinfill_none_p_kernel(
         lo = slice(0, HALF)
         hi = slice(HALF, P)
 
-        product(0, "a", slice(0, P))
-        evacuate(0, "y0")
+        halves = (slice(0, S // 2), slice(S // 2, S))
+        y[0] = keep.tile([P, S], F32, name="y0", align_bytes=64)
+        for h, cols in enumerate(halves):
+            acc = psum.tile([P, S // 2], F32, name="y_half%d" % h)
+            for i in range(2):
+                nc.tensor.matmul_mx(
+                    out=acc[:],
+                    lhsT=codes[i, "a"][:].bitcast(FP8X4),
+                    lhsT_scale=wscale[i, "a"][:],
+                    rhs=moving[i][0][:, cols].bitcast(FP8X4),
+                    rhs_scale=tok_scales[:, moving[i][1]][:, cols],
+                    start=(i == 0),
+                    stop=(i == 1),
+                )
+            nc.scalar.activation(y[0][:, cols], acc[:], COPY)
         send1(0)
 
-        w1_hi = load_half("w1_hi", "w1_raw", w1, 1)
-        w2_hi = load_half("w2_hi", "tok_bytes", w2, 1)
+        w1_hi = load_half("w1_hi", "g0a0", w1, 1, nc.sync)
+        w2_hi = load_half("w2_hi", "g0a1", w2, 1, nc.sync)
+        gain = keep.tile([P, PACK], F32, name="gain", tag="c1a", align_bytes=64)
+        nc.sync.dma_start(gain[:], gs.rearrange("(p t) o -> p (t o)", t=PACK))
         for i, raw in ((0, w1_hi), (1, w2_hi)):
-            nc.vector.tensor_copy(pair_view(i, "b"), by_slot(raw)[:, :, 0:2, :])
+            nc.vector.tensor_copy(pair_view(i, "b"), by_slot(raw)[:, :, 0:2, :][:, :, ::-1, :])
             quant(i, "b")
         larger_of(0, "g1b")
         send2(0)
@@ -197,8 +214,8 @@ def tile_picked_dthzksndtwinfill_none_p_kernel(
         send1(2)
 
         subtract(0, 1, "xh")
-        moved_lo = keep.tile([P, S], F32, name="moved_lo", align_bytes=64)
-        nc.sync.dma_start(moved_lo[lo, :], diff[0][hi, :])
+        moved = keep.tile([P, S], F32, name="moved", align_bytes=64)
+        nc.sync.dma_start(moved[lo, :], diff[0][hi, :])
         weigh(diff[0], 0, lo, allc)
         cand_bytes = keep.tile([P, C], U8, name="cand_bytes", tag="s1r", align_bytes=64)
         nc.vector.tensor_copy(cand_bytes[:], scale_rows[:].indirect(cand_t[:]))
@@ -210,27 +227,24 @@ def tile_picked_dthzksndtwinfill_none_p_kernel(
         send1(3)
         xc = keep.tile([P, C], U32, name="xc", tag="c1r", align_bytes=64)
         nc.vector.tensor_copy(xc[:], words[:].bitcast(U32).indirect(cand_t[:]))
-        weigh(moved_lo, 1, lo, allc)
         larger_of(2, "st2")
 
         subtract(1, 1, "diff1")
-        moved_hi = keep.tile([P, S], F32, name="moved_hi", align_bytes=64)
-        nc.sync.dma_start(moved_hi[hi, :], diff[1][lo, :])
-        weigh(diff[1], 1, hi, allc)
+        nc.sync.dma_start(moved[hi, :], diff[1][lo, :])
+        weigh(diff[1], 0, hi, allc)
         larger_of(3, "st3")
         send2(2)
         send2(3)
-        st3_weighed = keep.tile([P, S], F32, name="st3_weighed", align_bytes=64)
-        nc.vector.tensor_scalar(st3_weighed[:], st[3][:], gain[:, 3:4], None, ALU.mult)
-        weigh(moved_hi, 0, hi, allc)
-        subtract(2, 1, "moved_hi")
-        weigh(diff[2], 2, every, allc)
+        weigh(moved, 1, every, allc)
+        weighed = keep.tile([P, 2 * S], F32, name="weighed", tag="moved", align_bytes=64)
+        for r in (2, 3):
+            nc.vector.tensor_scalar(weighed[:, (r - 2) * S : (r - 1) * S], st[r][:], gain[:, r : r + 1], None, ALU.mult)
+        nc.vector.scalar_tensor_tensor(zb[:, :, 2], ds2[2][:, :S], gain[:, 2:3], weighed[:, :S], ALU.mult, ALU.subtract)
         zq = keep.tile([P, S], U32, name="zq", align_bytes=64)
         zs = keep.tile([P, S], U8, name="zs", align_bytes=64)
-        halves = (slice(0, S // 2), slice(S // 2, S))
         for cols in halves:
             nc.vector.scalar_tensor_tensor(
-                zb[:, cols, 3], ds2[3][:, cols], gain[:, 3:4], st3_weighed[:, cols], ALU.mult, ALU.subtract
+                zb[:, cols, 3], ds2[3][:, cols], gain[:, 3:4], weighed[:, S:][:, cols], ALU.mult, ALU.subtract
             )
         for cols in halves:
             nc.vector.quantize_mx(
@@ -254,13 +268,13 @@ def tile_picked_dthzksndtwinfill_none_p_kernel(
             s = keep.tile([P, S], F32, name="score%d" % c)
             if c == 0:
                 for h, cols in enumerate(halves):
-                    acc = psum.tile([P, S // 2], F32, name="s_half%d" % h, tag="y_acc%d" % h)
+                    acc = psum.tile([P, S // 2], F32, name="s_half%d" % h, tag="y_half%d" % h)
                     scores(acc[:], rows, cols)
-                    nc.scalar.activation(s[:, cols], acc[:], COPY)
+                    nc.scalar.activation(s[:, cols], acc[:], COPY, scale=-0.0625)
             else:
                 acc = psum.tile([P, S], F32, name="s_acc%d" % c)
                 scores(acc[:], rows, allc)
-                nc.vector.tensor_copy(s[:], acc[:])
+                nc.vector.tensor_scalar(s[:], acc[:], -0.0625, None, ALU.mult)
             score.append(s)
 
         larger = {}

from contextlib import ExitStack

import concourse.mybir as mybir

K, T, S, H, C, W = 512, 2048, 256, 512, 512, 128
FLOPS = 2 * K * H * S * 2 + 2 * K * C * S

F32 = mybir.dt.float32
BF16 = mybir.dt.bfloat16
I32 = mybir.dt.int32
U32 = mybir.dt.uint32
U16 = mybir.dt.uint16
U8 = mybir.dt.uint8
FP8X4 = mybir.dt.float8_e4m3fn_x4
ALU = mybir.AluOpType
COPY = mybir.ActivationFunctionType.Copy

P = 128
PACK = 4
HALF = P // 2
WINDOW = 2 * S


def tile_picked_dthzksndtwinfill_none_p_kernel(
    tc, x_words, x_scales, w1, w2, gs, offs, hz, n1, n2, cand, n3, n4, out
):
    nc = tc.nc
    with ExitStack() as ctx:
        lists = ctx.enter_context(tc.tile_pool(name="lists", bufs=1))
        keep = ctx.enter_context(tc.tile_pool(name="keep", bufs=1))
        psum = ctx.enter_context(tc.psum_pool(name="psum", bufs=1))

        def load_list(name, src):
            held = lists.tile(list(src.shape), U16, name=name)
            nc.sync.dma_start(held[:], src)
            return held

        def load_half(name, tag, w, half, queue):
            raw = keep.tile([P, PACK, S], F32, name=name, tag=tag, align_bytes=64)
            cols = slice(half * S, (half + 1) * S)
            queue.dma_start(raw[:], w.rearrange("(p j) c -> p j c", j=PACK)[:, :, cols])
            return raw

        w1_lo = load_half("w1_lo", "w1_raw", w1, 0, nc.scalar)
        scale_rows = keep.tile([P, T], U8, name="scale_rows")
        nc.vector.memset(scale_rows[:].bitcast(I32), 0)
        hz_t = load_list("hz_t", hz)
        offs_t = load_list("offs_t", offs)
        n1_t = load_list("n1_t", n1)
        for e in range(2):
            nc.sync.dma_start(
                scale_rows[e:P:16, :].bitcast(I32), x_scales[0, e:16:2, :].bitcast(I32)
            )
        words = keep.tile([P, T], I32, name="words")
        nc.sync.dma_start(words[:], x_words[0].rearrange("p n t -> p (n t)").bitcast(I32))
        w2_lo = load_half("w2_lo", "w2_raw", w2, 0, nc.sync)
        n2_t = load_list("n2_t", n2)
        cand_t = load_list("cand_t", cand)
        n3_t = load_list("n3_t", n3)
        n4_t = load_list("n4_t", n4)

        def place_scales(name, picked, queue):
            width = picked.shape[1]
            placed = keep.tile([P, width], U8, name=name, align_bytes=64)
            nc.vector.tensor_copy(placed[:].bitcast(I32), picked[:].bitcast(I32))
            for e in range(2):
                queue.dma_start(
                    placed[2 + e : P : 32, :].bitcast(I32), placed[16 + e : P : 32, :].bitcast(I32)
                )
            return placed

        tok_bytes = keep.tile([P, 2 * S], U8, name="tok_bytes", align_bytes=64)
        nc.vector.tensor_copy(tok_bytes[:, S:], scale_rows[:].indirect(hz_t[:]))
        nc.vector.tensor_copy(tok_bytes[:, :S], scale_rows[:].indirect(offs_t[:]))
        tok_scales = place_scales("tok_scales", tok_bytes, nc.sync)


        xq = keep.tile([P, S], U32, name="xq", align_bytes=64)
        nc.vector.tensor_copy(xq[:], words[:].bitcast(U32).indirect(offs_t[:]))
        xh = keep.tile([P, S], U32, name="xh", align_bytes=64)
        nc.vector.tensor_copy(xh[:], words[:].bitcast(U32).indirect(hz_t[:]))

        grouped = {}
        codes = {}
        wscale = {}
        for i in range(2):
            for name, width in (("a", P), ("b", P), ("r", 2 * P)):
                if name != "a":
                    grouped[i, name] = keep.tile([P, width * PACK], BF16, name="g%d%s" % (i, name), align_bytes=64)
                tag = "tok_bytes" if (i, name) == (0, "a") else "c%d%s" % (i, name)
                codes[i, name] = keep.tile([P, width], U32, name="c%d%s" % (i, name), tag=tag, align_bytes=64)
                wscale[i, name] = keep.tile([P, width], U8, name="s%d%s" % (i, name), align_bytes=64)

        def quant(i, name):
            nc.vector.quantize_mx(out=codes[i, name][:].bitcast(FP8X4), scales=wscale[i, name][:], in_=grouped[i, name][:])

        def by_slot(raw):
            return raw[:].rearrange("p j (m t) -> p m t j", t=PACK)

        def cast_cd(i, raw, half, engine):
            dst = grouped[i, "r"][:].rearrange("p (t m j) -> p m t j", t=2, j=PACK)[:, half * HALF : (half + 1) * HALF]
            src = by_slot(raw)[:, :, 2:4, :]
            if engine == "scalar":
                nc.scalar.activation(dst, src, COPY)
            else:
                nc.vector.tensor_copy(dst, src)

        def pair_view(i, name):
            return grouped[i, name][:].rearrange("p (t m j) -> p m t j", t=2, j=PACK)

        for i, raw in ((0, w1_lo), (1, w2_lo)):
            for t in range(2):
                one = keep.tile([P, HALF, PACK], BF16, name="g%da%d" % (i, t), align_bytes=64)
                if (i, t) == (1, 0):
                    nc.vector.tensor_copy(one[:], by_slot(raw)[:, :, t, :])
                else:
                    nc.scalar.activation(one[:], by_slot(raw)[:, :, t, :], COPY)
                cols = slice(t * HALF, (t + 1) * HALF)
                nc.vector.quantize_mx(
                    out=codes[i, "a"][:, cols].bitcast(FP8X4),
                    scales=wscale[i, "a"][:, cols],
                    in_=one[:].rearrange("p m j -> p (m j)"),
                )
            cast_cd(i, raw, 0, "scalar")

        moving = ((xq, slice(0, S)), (xh, slice(S, 2 * S)))
        acc_y = {}
        y = {}
        ds = {}
        st = {}
        ds2 = {}
        diff = {}

        def product(r, name, cols):
            acc_y[r] = psum.tile([P, S], F32, name="y_acc%d" % r)
            for i in range(2):
                nc.tensor.matmul_mx(
                    out=acc_y[r][:],
                    lhsT=codes[i, name][:, cols].bitcast(FP8X4),
                    lhsT_scale=wscale[i, name][:, cols],
                    rhs=moving[i][0][:].bitcast(FP8X4),
                    rhs_scale=tok_scales[:, moving[i][1]],
                    start=(i == 0),
                    stop=(i == 1),
                )

        def evacuate(r, tag):
            y[r] = keep.tile([P, S], F32, name="y%d" % r, tag=tag, align_bytes=64)
            nc.vector.tensor_copy(y[r][:], acc_y[r][:])

        def send1(r):
            ds[r] = keep.tile([P, WINDOW], F32, name="ds%d" % r, align_bytes=64)
            nc.scalar.activation(ds[r][:].indirect(n1_t[:]), y[r][:], COPY)

        def larger_of(r, tag):
            st[r] = keep.tile([P, S], F32, name="st%d" % r, tag=tag, align_bytes=64)
            nc.vector.tensor_tensor(st[r][:], ds[r][:, :S], y[r][:], ALU.max)

        def send2(r):
            ds2[r] = keep.tile([P, WINDOW], F32, name="ds2_%d" % r, align_bytes=64)
            nc.scalar.activation(ds2[r][:].indirect(n2_t[:]), st[r][:], COPY)

        def subtract(r, pieces, tag):
            diff[r] = keep.tile([P, S], F32, name="diff%d" % r, tag=tag, align_bytes=64)
            for h in range(pieces):
                cols = slice(h * S // pieces, (h + 1) * S // pieces)
                nc.vector.tensor_tensor(diff[r][:, cols], ds2[r][:, cols], st[r][:, cols], ALU.subtract)

        zb = keep.tile([P, S, PACK], BF16, name="zb", align_bytes=64)

        def weigh(src, slot, rows, cols):
            nc.vector.tensor_scalar(zb[rows, cols, slot], src[rows, cols], gain[rows, slot : slot + 1], None, ALU.mult)

        every = slice(0, P)
        allc = slice(0, S)
        lo = slice(0, HALF)
        hi = slice(HALF, P)

        halves = (slice(0, S // 2), slice(S // 2, S))
        y[0] = keep.tile([P, S], F32, name="y0", align_bytes=64)
        for h, cols in enumerate(halves):
            acc = psum.tile([P, S // 2], F32, name="y_half%d" % h)
            for i in range(2):
                nc.tensor.matmul_mx(
                    out=acc[:],
                    lhsT=codes[i, "a"][:].bitcast(FP8X4),
                    lhsT_scale=wscale[i, "a"][:],
                    rhs=moving[i][0][:, cols].bitcast(FP8X4),
                    rhs_scale=tok_scales[:, moving[i][1]][:, cols],
                    start=(i == 0),
                    stop=(i == 1),
                )
            nc.scalar.activation(y[0][:, cols], acc[:], COPY)
        send1(0)

        w1_hi = load_half("w1_hi", "g0a0", w1, 1, nc.sync)
        w2_hi = load_half("w2_hi", "g0a1", w2, 1, nc.sync)
        gain = keep.tile([P, PACK], F32, name="gain", tag="c1a", align_bytes=64)
        nc.sync.dma_start(gain[:], gs.rearrange("(p t) o -> p (t o)", t=PACK))
        for i, raw in ((0, w1_hi), (1, w2_hi)):
            nc.vector.tensor_copy(pair_view(i, "b"), by_slot(raw)[:, :, 0:2, :][:, :, ::-1, :])
            quant(i, "b")
        larger_of(0, "g1b")
        send2(0)
        product(1, "b", slice(0, P))
        evacuate(1, "y1")
        for i, raw in ((0, w1_hi), (1, w2_hi)):
            cast_cd(i, raw, 1, "vector")
            quant(i, "r")
        product(2, "r", slice(0, P))
        product(3, "r", slice(P, 2 * P))
        evacuate(2, "y2")
        send1(1)
        send1(2)

        subtract(0, 1, "xh")
        moved = keep.tile([P, S], F32, name="moved", align_bytes=64)
        nc.sync.dma_start(moved[lo, :], diff[0][hi, :])
        weigh(diff[0], 0, lo, allc)
        cand_bytes = keep.tile([P, C], U8, name="cand_bytes", tag="s1r", align_bytes=64)
        nc.vector.tensor_copy(cand_bytes[:], scale_rows[:].indirect(cand_t[:]))
        cand_scales = place_scales("cand_scales", cand_bytes, nc.sync)

        larger_of(1, "tok_scales")
        evacuate(3, "ds1")
        send2(1)
        send1(3)
        xc = keep.tile([P, C], U32, name="xc", tag="c1r", align_bytes=64)
        nc.vector.tensor_copy(xc[:], words[:].bitcast(U32).indirect(cand_t[:]))
        larger_of(2, "st2")

        subtract(1, 1, "diff1")
        nc.sync.dma_start(moved[hi, :], diff[1][lo, :])
        weigh(diff[1], 0, hi, allc)
        larger_of(3, "st3")
        send2(2)
        send2(3)
        weigh(moved, 1, every, allc)
        weighed = keep.tile([P, 2 * S], F32, name="weighed", tag="moved", align_bytes=64)
        for r in (2, 3):
            nc.vector.tensor_scalar(weighed[:, (r - 2) * S : (r - 1) * S], st[r][:], gain[:, r : r + 1], None, ALU.mult)
        nc.vector.scalar_tensor_tensor(zb[:, :, 2], ds2[2][:, :S], gain[:, 2:3], weighed[:, :S], ALU.mult, ALU.subtract)
        zq = keep.tile([P, S], U32, name="zq", align_bytes=64)
        zs = keep.tile([P, S], U8, name="zs", align_bytes=64)
        for cols in halves:
            nc.vector.scalar_tensor_tensor(
                zb[:, cols, 3], ds2[3][:, cols], gain[:, 3:4], weighed[:, S:][:, cols], ALU.mult, ALU.subtract
            )
        for cols in halves:
            nc.vector.quantize_mx(
                out=zq[:, cols].bitcast(FP8X4), scales=zs[:, cols], in_=zb[:, cols, :].rearrange("p n t -> p (n t)")
            )

        def scores(acc, rows, cols):
            nc.tensor.matmul_mx(
                out=acc,
                lhsT=xc[:, rows].bitcast(FP8X4),
                lhsT_scale=cand_scales[:, rows],
                rhs=zq[:, cols].bitcast(FP8X4),
                rhs_scale=zs[:, cols],
                start=True,
                stop=True,
            )

        score = []
        for c in range(C // P):
            rows = slice(c * P, (c + 1) * P)
            s = keep.tile([P, S], F32, name="score%d" % c)
            if c == 0:
                for h, cols in enumerate(halves):
                    acc = psum.tile([P, S // 2], F32, name="s_half%d" % h, tag="y_half%d" % h)
                    scores(acc[:], rows, cols)
                    nc.scalar.activation(s[:, cols], acc[:], COPY, scale=-0.0625)
            else:
                acc = psum.tile([P, S], F32, name="s_acc%d" % c)
                scores(acc[:], rows, allc)
                nc.vector.tensor_scalar(s[:], acc[:], -0.0625, None, ALU.mult)
            score.append(s)

        larger = {}

        def pair_up(c):
            pa = keep.tile([P, W], F32, name="pa%d" % c)
            pb = keep.tile([P, W], F32, name="pb%d" % c)
            nc.scalar.activation(pa[:], score[c][:].indirect(n3_t[:]), COPY)
            nc.scalar.activation(pb[:], score[c][:].indirect(n4_t[:]), COPY)
            larger[c] = keep.tile([P, W], F32, name="larger%d" % c)
            nc.vector.tensor_tensor(larger[c][:], pa[:], pb[:], ALU.max)

        def put_back(c):
            nc.scalar.activation(score[c][:].indirect(n3_t[:]), larger[c][:], COPY)
            queue = nc.scalar if c == C // P - 1 else nc.sync
            queue.dma_start(out[c * P : (c + 1) * P, :], score[c][:])

        pair_up(0)
        for c in range(1, C // P):
            pair_up(c)
            put_back(c - 1)
        put_back(C // P - 1)
